import numpy as np
import ml_dtypes


def mxq(x, axis, fmt="e4m3"):
    dtype, down = {"e4m3": (ml_dtypes.float8_e4m3fn, 7), "e5m2": (ml_dtypes.float8_e5m2, 14)}[fmt]
    v = np.moveaxis(np.asarray(x, np.float32).astype(ml_dtypes.bfloat16).astype(np.float64), axis, -1)
    blocks = v.reshape(v.shape[:-1] + (-1, 32))
    amax = np.abs(blocks).max(-1, keepdims=True)
    byte = np.maximum(np.where(amax > 0, np.frexp(amax)[1] - 1 + 127, 0) - down, 1)
    scale = np.exp2(byte - 127.0)
    codes = (blocks / scale).astype(np.float32).astype(dtype).astype(np.float64)
    return np.moveaxis((codes * scale).reshape(v.shape), -1, axis)


WIDE = False


def mx_kscale(k):
    if not WIDE:
        return np.ones(k)
    levels = np.array([30, -30])
    if k % 512:
        return np.exp2(np.random.permutation(np.resize(levels, k // 32))).repeat(32)
    a = np.empty((k // 512, 16))
    for p in range(k // 512):
        a[p, :8] = np.random.permutation(np.resize(levels, 8))
        for g in range(8):
            far = levels[np.abs(levels - a[p, g]) >= 10]
            a[p, g + 8] = far[np.random.randint(len(far))]
    return np.exp2(a.ravel()).repeat(32)


def f64(x):
    return np.asarray(x).astype(np.float64)


def striped(idx):
    return np.tile(np.asarray(idx).reshape(-1, 16).T, (8, 1)).astype(np.uint16)


def unstriped(offs):
    return offs[:16].T.reshape(-1).astype(np.int64)


E2M1 = np.array([0.0, 0.5, 1.0, 1.5, 2.0, 3.0, 4.0, 6.0, -0.0, -0.5, -1.0, -1.5, -2.0, -3.0, -4.0, -6.0])


def pack_weight(w, fmt):
    k, n = w.shape
    w = f64(np.asarray(w, np.float32).astype(ml_dtypes.bfloat16)).reshape(k // 32, 32, n)
    amax = np.abs(w).max(1)
    if fmt in ("e4m3", "e5m2"):
        byte = np.frexp(amax)[1] - 1 + 127 - (7 if fmt == "e4m3" else 14)
    else:
        mant, ex = np.frexp(amax / 6.0)
        byte = np.where(mant > 0.5, ex, ex - 1) + 127
    byte = np.clip(np.where(amax > 0, byte, 1), 1, 254)
    scaled = (w * np.exp2(127.0 - byte)[:, None, :]).reshape(k, n).astype(np.float32)
    by_word = np.ascontiguousarray(scaled.reshape(k // 512, 128, 4, n).transpose(0, 1, 3, 2))
    if fmt in ("e4m3", "e5m2"):
        words = by_word.astype(ml_dtypes.float8_e4m3fn if fmt == "e4m3" else ml_dtypes.float8_e5m2).view(np.uint8)
    else:
        c = by_word.astype(ml_dtypes.float4_e2m1fn).view(np.uint8) & 0xF
        words = (c[..., 0::2] | (c[..., 1::2] << 4)).reshape(k // 512, 128, 2 * n)
    return np.ascontiguousarray(words), np.ascontiguousarray(byte.astype(np.uint8).reshape(k // 512, 16, n))


def unpack_weight(words, scales, fmt):
    g, _, n = scales.shape
    words = np.ascontiguousarray(words).reshape(g, 128, n, -1)
    if fmt in ("e4m3", "e5m2"):
        vals = words.view(ml_dtypes.float8_e4m3fn if fmt == "e4m3" else ml_dtypes.float8_e5m2).astype(np.float64)
    else:
        nib = np.empty((g, 128, n, 4), np.uint8)
        nib[..., 0::2] = words & 0xF
        nib[..., 1::2] = words >> 4
        vals = E2M1[nib]
    vals = vals * np.repeat(np.exp2(scales.astype(np.float64) - 127.0), 8, axis=1)[..., None]
    return vals.transpose(0, 1, 3, 2).reshape(g * 512, n)


def e4m3fn_bytes(y):
    return np.clip(np.asarray(y, np.float64), -448.0, 448.0).astype(np.float32).astype(ml_dtypes.float8_e4m3fn).view(np.uint8)


def e4m3fn_values(b):
    return np.asarray(b, np.uint8).view(ml_dtypes.float8_e4m3fn).astype(np.float64)


K, T, J, R, F, Z, V, D, N = 512, 1024, 256, 512, 512, 1024, 1024, 512, 256


def setup_inputs():
    n = np.random.standard_normal
    idx = np.random.permutation(T)[:J]
    idx2 = np.random.permutation(Z)[:J]
    idx3 = np.random.permutation(V)[:J]
    idx4 = np.random.permutation(D)[:J]
    fk = mx_kscale(K)
    ff = mx_kscale(F)
    fr = mx_kscale(R)
    xtp = pack_weight(n((K, T)) / fk[:, None], "e4m3")
    xop = pack_weight(n((F, Z)) / ff[:, None], "e2m1")
    wp = pack_weight(n((K, R)) * 1 / np.sqrt(K) * fk[:, None] * fr, "e2m1")
    w0p = pack_weight(n((F, R)) * 1 / np.sqrt(F) * ff[:, None] * fr, "e5m2")
    wbp = pack_weight(n((R, N)) * 1 / np.sqrt(R) / fr[:, None], "e5m2")
    return {
        "xt_words": xtp[0],
        "xt_scales": xtp[1],
        "xo_words": xop[0],
        "xo_scales": xop[1],
        "w_words": wp[0],
        "w_scales": wp[1],
        "w0_words": w0p[0],
        "w0_scales": w0p[1],
        "wb_words": wbp[0],
        "wb_scales": wbp[1],
        "ca": e4m3fn_bytes(60.0 * n((N, V))),
        "cb": e4m3fn_bytes(60.0 * n((N, D))),
        "sa": (np.random.uniform(0.004, 0.012, (N, 1))).astype(np.float32),
        "sb": (np.random.uniform(0.004, 0.012, (N, 1))).astype(np.float32),
        "offs": striped(idx),
        "offs2": striped(idx2),
        "offs3": striped(idx3),
        "offs4": striped(idx4),
    }


def reference(xt_words, xt_scales, xo_words, xo_scales, w_words, w_scales, w0_words, w0_scales, wb_words, wb_scales, ca, cb, sa, sb, offs, offs2, offs3, offs4):
    idx = unstriped(offs)
    idx2 = unstriped(offs2)
    idx3 = unstriped(offs3)
    idx4 = unstriped(offs4)
    xtu = unpack_weight(xt_words, xt_scales, "e4m3")
    xou = unpack_weight(xo_words, xo_scales, "e2m1")
    wu = unpack_weight(w_words, w_scales, "e2m1")
    w0u = unpack_weight(w0_words, w0_scales, "e5m2")
    wbu = unpack_weight(wb_words, wb_scales, "e5m2")
    xtidxg = xtu[:, idx]
    xoidx2g = xou[:, idx2]
    a = wu.T @ xtidxg + w0u.T @ xoidx2g
    hid = np.maximum(a, 0.0)
    hidq = mxq(hid, 0, "e4m3")
    p = wbu.T @ hidq
    g1 = e4m3fn_values(ca)[:, idx3] * f64(sa)
    g2 = e4m3fn_values(cb)[:, idx4] * f64(sb)
    y = p * g1 + g2
    return y

@@ -1,0 +1,178 @@
+from contextlib import ExitStack
+
+import concourse.mybir as mybir
+
+K, T, J, R, F, Z, V, D, N = 512, 1024, 256, 512, 512, 1024, 1024, 512, 256
+FLOPS = 2 * (K * R * J + F * R * J + R * N * J)
+
+F32 = mybir.dt.float32
+BF16 = mybir.dt.bfloat16
+I32 = mybir.dt.int32
+U32 = mybir.dt.uint32
+U16 = mybir.dt.uint16
+U8 = mybir.dt.uint8
+E4M3 = mybir.dt.float8_e4m3fn
+E4M3X4 = mybir.dt.float8_e4m3fn_x4
+E5M2X4 = mybir.dt.float8_e5m2_x4
+E2M1X4 = mybir.dt.float4_e2m1fn_x4
+ACT = mybir.ActivationFunctionType
+ALU = mybir.AluOpType
+
+P = 128
+PACK = 4
+HALF = J // 2
+
+
+def load_rows(queue, plane, scales, q):
+    queue.dma_start(plane[32 * q : 32 * q + 4, :].bitcast(I32), scales[0, 4 * q : 4 * q + 4, :].bitcast(I32))
+
+
+def tile_list_gainandshift_kernel(
+    tc, xt_words, xt_scales, xo_words, xo_scales, w_words, w_scales, w0_words, w0_scales,
+    wb_words, wb_scales, ca, cb, sa, sb, offs, offs2, offs3, offs4, out,
+):
+    nc = tc.nc
+    with ExitStack() as ctx:
+        lists = ctx.enter_context(tc.tile_pool(name="lists", bufs=1))
+        keep = ctx.enter_context(tc.tile_pool(name="keep", bufs=1))
+        psum = ctx.enter_context(tc.psum_pool(name="psum", bufs=1))
+
+        def sb_tile(name, shape, dtype):
+            return keep.tile(shape, dtype, name=name, align_bytes=64)
+
+        idx_t = lists.tile([P, J // 16], U16, name="idx_t")
+        idx_o = lists.tile([P, J // 16], U16, name="idx_o")
+        idx_a = lists.tile([P, J // 16], U16, name="idx_a")
+        idx_b = lists.tile([P, J // 16], U16, name="idx_b")
+
+        xt_w = sb_tile("xt_w", [P, T], U32)
+        xt_s = sb_tile("xt_s", [P, T], U8)
+        xo_w = sb_tile("xo_w", [P, Z], U16)
+        xo_s = sb_tile("xo_s", [P, Z], U8)
+        w_w = sb_tile("w_w", [P, R], U16)
+        w_s = sb_tile("w_s", [P, R], U8)
+        w0_w = sb_tile("w0_w", [P, R], U32)
+        w0_s = sb_tile("w0_s", [P, R], U8)
+        wb_w = sb_tile("wb_w", [P, N], U32)
+        wb_s = sb_tile("wb_s", [P, N], U8)
+        ca_t = [sb_tile("ca_%d" % n, [P, V], U8) for n in range(2)]
+        cb_t = [sb_tile("cb_%d" % n, [P, D], U8) for n in range(2)]
+        sa_t = sb_tile("sa_t", [P, 2], F32)
+        sb_t = sb_tile("sb_t", [P, 2], F32)
+
+        for plane in (xt_s, xo_s, w0_s):
+            nc.vector.memset(plane[:].bitcast(I32), 0)
+        for plane in (w_s, wb_s):
+            nc.gpsimd.memset(plane[:].bitcast(I32), 0)
+
+        nc.sync.dma_start(idx_t[:], offs)
+        nc.sync.dma_start(xt_w[:].bitcast(I32), xt_words[0].rearrange("p n t -> p (n t)").bitcast(I32))
+        for q in range(4):
+            load_rows(nc.scalar, xt_s, xt_scales, q)
+        nc.sync.dma_start(idx_o[:], offs2)
+        nc.sync.dma_start(xo_w[:].bitcast(I32), xo_words[0].bitcast(I32))
+        for q in range(2):
+            load_rows(nc.gpsimd, w_s, w_scales, q)
+        nc.scalar.dma_start(w_w[:].bitcast(I32), w_words[0].bitcast(I32))
+        for q in range(2, 4):
+            load_rows(nc.scalar, w_s, w_scales, q)
+        for q in range(4):
+            load_rows(nc.sync, xo_s, xo_scales, q)
+        nc.scalar.dma_start(w0_w[:].bitcast(I32), w0_words[0].rearrange("p n t -> p (n t)").bitcast(I32))
+        for q in range(2):
+            load_rows(nc.gpsimd, w0_s, w0_scales, q)
+        for q in range(2, 4):
+            load_rows(nc.sync, w0_s, w0_scales, q)
+        nc.sync.dma_start(idx_a[:], offs3)
+        for n in range(2):
+            nc.sync.dma_start(ca_t[n][:], ca[n * P : (n + 1) * P, :])
+        nc.sync.dma_start(idx_b[:], offs4)
+        for n in range(2):
+            nc.sync.dma_start(cb_t[n][:], cb[n * P : (n + 1) * P, :])
+        nc.sync.dma_start(wb_w[:].bitcast(I32), wb_words[0].rearrange("p n t -> p (n t)").bitcast(I32))
+        for q in range(4):
+            load_rows(nc.sync, wb_s, wb_scales, q)
+        with nc.allow_non_contiguous_dma(reason="one step a partition"):
+            nc.gpsimd.dma_start(sa_t[:], sa.rearrange("(n p) o -> p (n o)", p=P))
+            nc.gpsimd.dma_start(sb_t[:], sb.rearrange("(n p) o -> p (n o)", p=P))
+
+        w_wd = sb_tile("w_wd", [P, PACK, P], U16)
+        w_sd = sb_tile("w_sd", [P, PACK, P], U8)
+        w0_wd = sb_tile("w0_wd", [P, PACK, P], U32)
+        w0_sd = sb_tile("w0_sd", [P, PACK, P], U8)
+
+        def dealt(tile):
+            return tile[:].rearrange("p (m t) -> p t m", t=PACK)
+
+        xt_wg = sb_tile("xt_wg", [P, J], U32)
+        xt_sg = sb_tile("xt_sg", [P, J], U8)
+        xo_wg = sb_tile("xo_wg", [P, J], U16)
+        xo_sg = sb_tile("xo_sg", [P, J], U8)
+
+        nc.vector.tensor_copy(xt_sg[:], xt_s[:].indirect(idx_t[:]))
+        nc.vector.tensor_copy(xt_wg[:], xt_w[:].indirect(idx_t[:]))
+        nc.scalar.copy(w_wd[:], dealt(w_w))
+        nc.vector.tensor_copy(w_sd[:], dealt(w_s))
+        nc.vector.tensor_copy(xo_wg[:], xo_w[:].indirect(idx_o[:]))
+        nc.vector.tensor_copy(xo_sg[:], xo_s[:].indirect(idx_o[:]))
+        nc.scalar.copy(w0_wd[:], dealt(w0_w))
+        nc.vector.tensor_copy(w0_sd[:], dealt(w0_s))
+
+        a_ps = [psum.tile([P, PACK, HALF], F32, name="a_ps%d" % h) for h in range(2)]
+        p_ps = [psum.tile([P, 2, HALF], F32, name="p_ps%d" % h) for h in range(2)]
+        halves = [slice(h * HALF, (h + 1) * HALF) for h in range(2)]
+
+        for h in range(2):
+            for t in range(PACK):
+                nc.tensor.matmul_mx(
+                    out=a_ps[h][:, t, :], lhsT=w_wd[:, t, :].bitcast(E2M1X4), lhsT_scale=w_sd[:, t, :],
+                    rhs=xt_wg[:, halves[h]].bitcast(E4M3X4), rhs_scale=xt_sg[:, halves[h]],
+                    start=(t == 0), stop=False,
+                )
+        for h in range(2):
+            for t in range(PACK):
+                nc.tensor.matmul_mx(
+                    out=a_ps[h][:, t, :], lhsT=w0_wd[:, t, :].bitcast(E5M2X4), lhsT_scale=w0_sd[:, t, :],
+                    rhs=xo_wg[:, halves[h]].bitcast(E2M1X4), rhs_scale=xo_sg[:, halves[h]],
+                    start=False, stop=(t == PACK - 1),
+                )
+
+        ca_g = sb_tile("ca_g", [P, 2, J], U8)
+        cb_g = sb_tile("cb_g", [P, 2, J], U8)
+        gain = sb_tile("gain", [P, 2, J], F32)
+        shift = sb_tile("shift", [P, 2, J], F32)
+        hid = [sb_tile("hid%d" % h, [P, HALF, PACK], BF16) for h in range(2)]
+        hid_w = [sb_tile("hid_w%d" % h, [P, HALF], U32) for h in range(2)]
+        hid_s = [sb_tile("hid_s%d" % h, [P, HALF], U8) for h in range(2)]
+
+        for n in range(2):
+            nc.vector.tensor_copy(ca_g[:, n, :], ca_t[n][:].indirect(idx_a[:]))
+        for h in range(2):
+            nc.scalar.activation(hid[h][:], a_ps[h][:].rearrange("p t j -> p j t"), ACT.Relu)
+        for n in range(2):
+            nc.vector.tensor_copy(cb_g[:, n, :], cb_t[n][:].indirect(idx_b[:]))
+        for h in range(2):
+            nc.vector.quantize_mx(
+                out=hid_w[h][:].bitcast(E4M3X4), scales=hid_s[h][:], in_=hid[h][:].rearrange("p j t -> p (j t)")
+            )
+        for n in range(2):
+            nc.scalar.activation(gain[:, n, :], ca_g[:, n, :].bitcast(E4M3), ACT.Copy, scale=sa_t[:, n : n + 1])
+        for n in range(2):
+            nc.scalar.activation(shift[:, n, :], cb_g[:, n, :].bitcast(E4M3), ACT.Copy, scale=sb_t[:, n : n + 1])
+
+        for h in range(2):
+            for n in range(2):
+                cols = slice(n * P, (n + 1) * P)
+                nc.tensor.matmul_mx(
+                    out=p_ps[h][:, n, :], lhsT=wb_w[:, cols].bitcast(E5M2X4), lhsT_scale=wb_s[:, cols],
+                    rhs=hid_w[h][:].bitcast(E4M3X4), rhs_scale=hid_s[h][:], start=True, stop=True,
+                )
+
+        out_v = out.rearrange("(n p) j -> p n j", p=P)
+        scaled = [sb_tile("scaled%d" % h, [P, 2, HALF], F32) for h in range(2)]
+        result = [sb_tile("result%d" % h, [P, 2, HALF], F32) for h in range(2)]
+        for h in range(2):
+            nc.vector.tensor_tensor(scaled[h][:], p_ps[h][:], gain[:, :, halves[h]], ALU.mult)
+        for h in range(2):
+            nc.vector.tensor_tensor(result[h][:], scaled[h][:], shift[:, :, halves[h]], ALU.add)
+            nc.sync.dma_start(out_v[:, :, halves[h]], result[h][:])

@@ -23,8 +23,36 @@ PACK = 4
 HALF = J // 2
 
 
+def load_filled(queue, plane, scales, q):
+    rows = scales[0, 4 * q : 4 * q + 4, :].bitcast(I32)
+    queue.dma_start(plane[32 * q : 32 * q + 32, :].bitcast(I32), rows.unsqueeze(0).broadcast_to([8, 4, rows.shape[1]]))
+
+
 def load_rows(queue, plane, scales, q):
     queue.dma_start(plane[32 * q : 32 * q + 4, :].bitcast(I32), scales[0, 4 * q : 4 * q + 4, :].bitcast(I32))
+
+
+def load_pair(queue, stage, scales, q):
+    rows = scales[0].bitcast(I32).rearrange("(u q r) c -> q r u c", u=2, q=2)
+    queue.dma_start(stage[32 * q : 32 * q + 4, :, :].bitcast(I32), rows[q])
+
+
+def load_staged(queue, stage, scales):
+    queue.dma_start(stage[0:4, :, :].bitcast(I32), scales[0].bitcast(I32).rearrange("(q r) c -> r q c", r=4))
+
+
+def load_steps(nc, queue, tile, steps):
+    with nc.allow_non_contiguous_dma(reason="one step a partition"):
+        queue.dma_start(tile[:], steps.rearrange("(n p) o -> p (n o)", p=P))
+
+
+def lift(nc, stage):
+    nc.vector.tensor_copy(stage[64:128, 0, :].bitcast(I32), stage[0:64, 1, :].bitcast(I32))
+
+
+def spread(nc, plane, stage, quadrants):
+    for q in quadrants:
+        nc.vector.tensor_copy(plane[32 * q : 32 * q + 4, :].bitcast(I32), stage[0:4, q, :].bitcast(I32))
 
 
 def tile_list_gainandshift_kernel(
@@ -37,8 +65,8 @@ def tile_list_gainandshift_kernel(
         keep = ctx.enter_context(tc.tile_pool(name="keep", bufs=1))
         psum = ctx.enter_context(tc.psum_pool(name="psum", bufs=1))
 
-        def sb_tile(name, shape, dtype):
-            return keep.tile(shape, dtype, name=name, align_bytes=64)
+        def sb_tile(name, shape, dtype, tag=None):
+            return keep.tile(shape, dtype, name=name, tag=tag or name, align_bytes=64)
 
         idx_t = lists.tile([P, J // 16], U16, name="idx_t")
         idx_o = lists.tile([P, J // 16], U16, name="idx_o")
@@ -60,49 +88,54 @@ def tile_list_gainandshift_kernel(
         sa_t = sb_tile("sa_t", [P, 2], F32)
         sb_t = sb_tile("sb_t", [P, 2], F32)
 
-        for plane in (xt_s, xo_s, w0_s):
-            nc.vector.memset(plane[:].bitcast(I32), 0)
-        for plane in (w_s, wb_s):
-            nc.gpsimd.memset(plane[:].bitcast(I32), 0)
+        nc.vector.memset(xt_s[:].bitcast(I32), 0)
+        nc.vector.memset(w_s[64:128, :].bitcast(I32), 0)
+        nc.vector.memset(xo_s[:].bitcast(I32), 0)
+        nc.vector.memset(w0_s[64:128, :].bitcast(I32), 0)
 
         nc.sync.dma_start(idx_t[:], offs)
-        nc.sync.dma_start(xt_w[:].bitcast(I32), xt_words[0].rearrange("p n t -> p (n t)").bitcast(I32))
-        for q in range(4):
-            load_rows(nc.scalar, xt_s, xt_scales, q)
-        nc.sync.dma_start(idx_o[:], offs2)
-        nc.sync.dma_start(xo_w[:].bitcast(I32), xo_words[0].bitcast(I32))
-        for q in range(2):
-            load_rows(nc.gpsimd, w_s, w_scales, q)
         nc.scalar.dma_start(w_w[:].bitcast(I32), w_words[0].bitcast(I32))
-        for q in range(2, 4):
-            load_rows(nc.scalar, w_s, w_scales, q)
-        for q in range(4):
-            load_rows(nc.sync, xo_s, xo_scales, q)
-        nc.scalar.dma_start(w0_w[:].bitcast(I32), w0_words[0].rearrange("p n t -> p (n t)").bitcast(I32))
-        for q in range(2):
-            load_rows(nc.gpsimd, w0_s, w0_scales, q)
-        for q in range(2, 4):
-            load_rows(nc.sync, w0_s, w0_scales, q)
+        load_rows(nc.sync, xt_s, xt_scales, 0)
+        load_rows(nc.scalar, xt_s, xt_scales, 2)
+        load_rows(nc.sync, xt_s, xt_scales, 1)
+        load_rows(nc.scalar, xt_s, xt_scales, 3)
+        nc.sync.dma_start(idx_o[:], offs2)
+        nc.sync.dma_start(xt_w[:].bitcast(I32), xt_words[0].rearrange("p n t -> p (n t)").bitcast(I32))
+        load_filled(nc.gpsimd, w_s, w_scales, 0)
+        load_filled(nc.gpsimd, w0_s, w0_scales, 0)
+        load_filled(nc.gpsimd, w0_s, w0_scales, 1)
+        load_filled(nc.sync, w_s, w_scales, 1)
+        load_rows(nc.sync, w_s, w_scales, 2)
+        load_rows(nc.sync, w_s, w_scales, 3)
+        nc.sync.dma_start(xo_w[:].bitcast(I32), xo_words[0].bitcast(I32))
+        load_rows(nc.sync, xo_s, xo_scales, 0)
+        load_rows(nc.sync, xo_s, xo_scales, 1)
+        load_rows(nc.sync, xo_s, xo_scales, 2)
+        load_rows(nc.sync, xo_s, xo_scales, 3)
+        nc.sync.dma_start(w0_w[:].bitcast(I32), w0_words[0].rearrange("p n t -> p (n t)").bitcast(I32))
+        load_rows(nc.sync, w0_s, w0_scales, 2)
+        load_rows(nc.sync, w0_s, w0_scales, 3)
         nc.sync.dma_start(idx_a[:], offs3)
-        for n in range(2):
-            nc.sync.dma_start(ca_t[n][:], ca[n * P : (n + 1) * P, :])
+        nc.sync.dma_start(ca_t[0][:], ca[0:P, :])
+        nc.sync.dma_start(ca_t[1][:], ca[P : 2 * P, :])
         nc.sync.dma_start(idx_b[:], offs4)
-        for n in range(2):
-            nc.sync.dma_start(cb_t[n][:], cb[n * P : (n + 1) * P, :])
+        nc.sync.dma_start(cb_t[0][:], cb[0:P, :])
+        nc.sync.dma_start(cb_t[1][:], cb[P : 2 * P, :])
         nc.sync.dma_start(wb_w[:].bitcast(I32), wb_words[0].rearrange("p n t -> p (n t)").bitcast(I32))
-        for q in range(4):
-            load_rows(nc.sync, wb_s, wb_scales, q)
-        with nc.allow_non_contiguous_dma(reason="one step a partition"):
-            nc.gpsimd.dma_start(sa_t[:], sa.rearrange("(n p) o -> p (n o)", p=P))
-            nc.gpsimd.dma_start(sb_t[:], sb.rearrange("(n p) o -> p (n o)", p=P))
+        load_rows(nc.sync, wb_s, wb_scales, 0)
+        load_rows(nc.sync, wb_s, wb_scales, 1)
+        load_rows(nc.sync, wb_s, wb_scales, 2)
+        load_rows(nc.sync, wb_s, wb_scales, 3)
+        load_steps(nc, nc.gpsimd, sa_t, sa)
+        load_steps(nc, nc.gpsimd, sb_t, sb)
 
         w_wd = sb_tile("w_wd", [P, PACK, P], U16)
         w_sd = sb_tile("w_sd", [P, PACK, P], U8)
-        w0_wd = sb_tile("w0_wd", [P, PACK, P], U32)
+        w0_wd = sb_tile("w0_wd", [P, PACK, P], U32, tag="w0_then_steps")
         w0_sd = sb_tile("w0_sd", [P, PACK, P], U8)
 
-        def dealt(tile):
-            return tile[:].rearrange("p (m t) -> p t m", t=PACK)
+        def dealt(rows):
+            return rows.rearrange("p (m t) -> p t m", t=PACK)
 
         xt_wg = sb_tile("xt_wg", [P, J], U32)
         xt_sg = sb_tile("xt_sg", [P, J], U8)
@@ -111,12 +144,12 @@ def tile_list_gainandshift_kernel(
 
         nc.vector.tensor_copy(xt_sg[:], xt_s[:].indirect(idx_t[:]))
         nc.vector.tensor_copy(xt_wg[:], xt_w[:].indirect(idx_t[:]))
-        nc.scalar.copy(w_wd[:], dealt(w_w))
-        nc.vector.tensor_copy(w_sd[:], dealt(w_s))
+        nc.scalar.copy(w_wd[:], dealt(w_w[:]))
+        nc.vector.tensor_copy(w_sd[:], dealt(w_s[:]))
         nc.vector.tensor_copy(xo_wg[:], xo_w[:].indirect(idx_o[:]))
         nc.vector.tensor_copy(xo_sg[:], xo_s[:].indirect(idx_o[:]))
-        nc.scalar.copy(w0_wd[:], dealt(w0_w))
-        nc.vector.tensor_copy(w0_sd[:], dealt(w0_s))
+        nc.scalar.copy(w0_wd[:], dealt(w0_w[:]))
+        nc.vector.tensor_copy(w0_sd[:], dealt(w0_s[:]))
 
         a_ps = [psum.tile([P, PACK, HALF], F32, name="a_ps%d" % h) for h in range(2)]
         p_ps = [psum.tile([P, 2, HALF], F32, name="p_ps%d" % h) for h in range(2)]
@@ -137,28 +170,29 @@ def tile_list_gainandshift_kernel(
                     start=False, stop=(t == PACK - 1),
                 )
 
-        ca_g = sb_tile("ca_g", [P, 2, J], U8)
-        cb_g = sb_tile("cb_g", [P, 2, J], U8)
-        gain = sb_tile("gain", [P, 2, J], F32)
-        shift = sb_tile("shift", [P, 2, J], F32)
+        ca_g = [sb_tile("ca_g%d" % n, [P, J], U8) for n in range(2)]
+        cb_g = [sb_tile("cb_g%d" % n, [P, J], U8) for n in range(2)]
+        looked_up = sb_tile("looked_up", [P, 4 * J], F32, tag="w0_then_steps")
+        gain = looked_up[:, 0 : 2 * J].rearrange("p (n j) -> p n j", n=2)
+        shift = looked_up[:, 2 * J : 4 * J].rearrange("p (n j) -> p n j", n=2)
         hid = [sb_tile("hid%d" % h, [P, HALF, PACK], BF16) for h in range(2)]
         hid_w = [sb_tile("hid_w%d" % h, [P, HALF], U32) for h in range(2)]
         hid_s = [sb_tile("hid_s%d" % h, [P, HALF], U8) for h in range(2)]
 
         for n in range(2):
-            nc.vector.tensor_copy(ca_g[:, n, :], ca_t[n][:].indirect(idx_a[:]))
+            nc.vector.tensor_copy(ca_g[n][:], ca_t[n][:].indirect(idx_a[:]))
         for h in range(2):
             nc.scalar.activation(hid[h][:], a_ps[h][:].rearrange("p t j -> p j t"), ACT.Relu)
         for n in range(2):
-            nc.vector.tensor_copy(cb_g[:, n, :], cb_t[n][:].indirect(idx_b[:]))
+            nc.vector.tensor_copy(cb_g[n][:], cb_t[n][:].indirect(idx_b[:]))
         for h in range(2):
             nc.vector.quantize_mx(
                 out=hid_w[h][:].bitcast(E4M3X4), scales=hid_s[h][:], in_=hid[h][:].rearrange("p j t -> p (j t)")
             )
         for n in range(2):
-            nc.scalar.activation(gain[:, n, :], ca_g[:, n, :].bitcast(E4M3), ACT.Copy, scale=sa_t[:, n : n + 1])
+            nc.scalar.activation(looked_up[:, n * J : (n + 1) * J], ca_g[n][:].bitcast(E4M3), ACT.Copy, scale=sa_t[:, n : n + 1])
         for n in range(2):
-            nc.scalar.activation(shift[:, n, :], cb_g[:, n, :].bitcast(E4M3), ACT.Copy, scale=sb_t[:, n : n + 1])
+            nc.scalar.activation(looked_up[:, (2 + n) * J : (3 + n) * J], cb_g[n][:].bitcast(E4M3), ACT.Copy, scale=sb_t[:, n : n + 1])
 
         for h in range(2):
             for n in range(2):

@@ -76,7 +76,7 @@ def tile_list_gainandshift_kernel(
         xt_w = sb_tile("xt_w", [P, T], U32)
         xt_s = sb_tile("xt_s", [P, T], U8)
         xo_w = sb_tile("xo_w", [P, Z], U16)
-        xo_s = sb_tile("xo_s", [P, Z], U8)
+        xo_s = sb_tile("xo_s", [P, Z], U8, tag="xo_then_w0")
         w_w = sb_tile("w_w", [P, R], U16)
         w_s = sb_tile("w_s", [P, R], U8)
         w0_w = sb_tile("w0_w", [P, R], U32)
@@ -88,23 +88,23 @@ def tile_list_gainandshift_kernel(
         sa_t = sb_tile("sa_t", [P, 2], F32)
         sb_t = sb_tile("sb_t", [P, 2], F32)
 
-        nc.vector.memset(xt_s[:].bitcast(I32), 0)
-        nc.vector.memset(w_s[64:128, :].bitcast(I32), 0)
+        nc.vector.memset(w_s[:].bitcast(I32), 0)
         nc.vector.memset(xo_s[:].bitcast(I32), 0)
-        nc.vector.memset(w0_s[64:128, :].bitcast(I32), 0)
 
         nc.sync.dma_start(idx_t[:], offs)
+        load_filled(nc.scalar, xt_s, xt_scales, 2)
+        load_filled(nc.sync, xt_s, xt_scales, 0)
+        load_filled(nc.scalar, xt_s, xt_scales, 3)
+        load_filled(nc.sync, xt_s, xt_scales, 1)
         nc.scalar.dma_start(w_w[:].bitcast(I32), w_words[0].bitcast(I32))
-        load_rows(nc.sync, xt_s, xt_scales, 0)
-        load_rows(nc.scalar, xt_s, xt_scales, 2)
-        load_rows(nc.sync, xt_s, xt_scales, 1)
-        load_rows(nc.scalar, xt_s, xt_scales, 3)
         nc.sync.dma_start(idx_o[:], offs2)
         nc.sync.dma_start(xt_w[:].bitcast(I32), xt_words[0].rearrange("p n t -> p (n t)").bitcast(I32))
-        load_filled(nc.gpsimd, w_s, w_scales, 0)
+        nc.gpsimd.dma_start(w0_w[:].bitcast(I32), w0_words[0].rearrange("p n t -> p (n t)").bitcast(I32))
         load_filled(nc.gpsimd, w0_s, w0_scales, 0)
         load_filled(nc.gpsimd, w0_s, w0_scales, 1)
-        load_filled(nc.sync, w_s, w_scales, 1)
+        load_filled(nc.gpsimd, w0_s, w0_scales, 2)
+        load_rows(nc.sync, w_s, w_scales, 0)
+        load_rows(nc.sync, w_s, w_scales, 1)
         load_rows(nc.sync, w_s, w_scales, 2)
         load_rows(nc.sync, w_s, w_scales, 3)
         nc.sync.dma_start(xo_w[:].bitcast(I32), xo_words[0].bitcast(I32))
@@ -112,9 +112,7 @@ def tile_list_gainandshift_kernel(
         load_rows(nc.sync, xo_s, xo_scales, 1)
         load_rows(nc.sync, xo_s, xo_scales, 2)
         load_rows(nc.sync, xo_s, xo_scales, 3)
-        nc.sync.dma_start(w0_w[:].bitcast(I32), w0_words[0].rearrange("p n t -> p (n t)").bitcast(I32))
-        load_rows(nc.sync, w0_s, w0_scales, 2)
-        load_rows(nc.sync, w0_s, w0_scales, 3)
+        load_filled(nc.sync, w0_s, w0_scales, 3)
         nc.sync.dma_start(idx_a[:], offs3)
         nc.sync.dma_start(ca_t[0][:], ca[0:P, :])
         nc.sync.dma_start(ca_t[1][:], ca[P : 2 * P, :])
@@ -122,17 +120,17 @@ def tile_list_gainandshift_kernel(
         nc.sync.dma_start(cb_t[0][:], cb[0:P, :])
         nc.sync.dma_start(cb_t[1][:], cb[P : 2 * P, :])
         nc.sync.dma_start(wb_w[:].bitcast(I32), wb_words[0].rearrange("p n t -> p (n t)").bitcast(I32))
+        load_steps(nc, nc.sync, sa_t, sa)
         load_rows(nc.sync, wb_s, wb_scales, 0)
         load_rows(nc.sync, wb_s, wb_scales, 1)
         load_rows(nc.sync, wb_s, wb_scales, 2)
         load_rows(nc.sync, wb_s, wb_scales, 3)
-        load_steps(nc, nc.gpsimd, sa_t, sa)
-        load_steps(nc, nc.gpsimd, sb_t, sb)
+        load_steps(nc, nc.sync, sb_t, sb)
 
         w_wd = sb_tile("w_wd", [P, PACK, P], U16)
         w_sd = sb_tile("w_sd", [P, PACK, P], U8)
         w0_wd = sb_tile("w0_wd", [P, PACK, P], U32, tag="w0_then_steps")
-        w0_sd = sb_tile("w0_sd", [P, PACK, P], U8)
+        w0_sd = sb_tile("w0_sd", [P, PACK, P], U8, tag="xo_then_w0")
 
         def dealt(rows):
             return rows.rearrange("p (m t) -> p t m", t=PACK)
@@ -144,11 +142,11 @@ def tile_list_gainandshift_kernel(
 
         nc.vector.tensor_copy(xt_sg[:], xt_s[:].indirect(idx_t[:]))
         nc.vector.tensor_copy(xt_wg[:], xt_w[:].indirect(idx_t[:]))
-        nc.scalar.copy(w_wd[:], dealt(w_w[:]))
+        nc.scalar.copy(w_wd[:].rearrange("p t m -> p m t"), w_w[:].rearrange("p (m t) -> p m t", t=PACK))
         nc.vector.tensor_copy(w_sd[:], dealt(w_s[:]))
         nc.vector.tensor_copy(xo_wg[:], xo_w[:].indirect(idx_o[:]))
         nc.vector.tensor_copy(xo_sg[:], xo_s[:].indirect(idx_o[:]))
-        nc.scalar.copy(w0_wd[:], dealt(w0_w[:]))
+        nc.scalar.copy(w0_wd[:].rearrange("p t m -> p m t"), w0_w[:].rearrange("p (m t) -> p m t", t=PACK))
         nc.vector.tensor_copy(w0_sd[:], dealt(w0_s[:]))
 
         a_ps = [psum.tile([P, PACK, HALF], F32, name="a_ps%d" % h) for h in range(2)]

@@ -75,12 +75,12 @@ def tile_list_gainandshift_kernel(
 
         xt_w = sb_tile("xt_w", [P, T], U32)
         xt_s = sb_tile("xt_s", [P, T], U8)
-        xo_w = sb_tile("xo_w", [P, Z], U16)
-        xo_s = sb_tile("xo_s", [P, Z], U8, tag="xo_then_w0")
+        xo_w = sb_tile("xo_w", [P, Z], U16, tag="xo_then_w0")
+        xo_s = sb_tile("xo_s", [P, Z], U8)
         w_w = sb_tile("w_w", [P, R], U16)
-        w_s = sb_tile("w_s", [P, R], U8)
+        w_s = sb_tile("w_s", [P, 2, R], U8)
         w0_w = sb_tile("w0_w", [P, R], U32)
-        w0_s = sb_tile("w0_s", [P, R], U8)
+        w0_s = sb_tile("w0_s", [P, 2, R], U8)
         wb_w = sb_tile("wb_w", [P, N], U32)
         wb_s = sb_tile("wb_s", [P, N], U8)
         ca_t = [sb_tile("ca_%d" % n, [P, V], U8) for n in range(2)]
@@ -88,7 +88,8 @@ def tile_list_gainandshift_kernel(
         sa_t = sb_tile("sa_t", [P, 2], F32)
         sb_t = sb_tile("sb_t", [P, 2], F32)
 
-        nc.vector.memset(w_s[:].bitcast(I32), 0)
+        nc.vector.memset(w_s[:].rearrange("p u c -> p (u c)").bitcast(I32), 0)
+        nc.vector.memset(w0_s[:].rearrange("p u c -> p (u c)").bitcast(I32), 0)
         nc.vector.memset(xo_s[:].bitcast(I32), 0)
 
         nc.sync.dma_start(idx_t[:], offs)
@@ -96,36 +97,32 @@ def tile_list_gainandshift_kernel(
         load_filled(nc.sync, xt_s, xt_scales, 0)
         load_filled(nc.scalar, xt_s, xt_scales, 3)
         load_filled(nc.sync, xt_s, xt_scales, 1)
-        nc.scalar.dma_start(w_w[:].bitcast(I32), w_words[0].bitcast(I32))
-        nc.sync.dma_start(idx_o[:], offs2)
+        load_pair(nc.scalar, w_s, w_scales, 0)
+        load_pair(nc.sync, w_s, w_scales, 1)
         nc.sync.dma_start(xt_w[:].bitcast(I32), xt_words[0].rearrange("p n t -> p (n t)").bitcast(I32))
+        nc.gpsimd.dma_start(w_w[:].bitcast(I32), w_words[0].bitcast(I32))
         nc.gpsimd.dma_start(w0_w[:].bitcast(I32), w0_words[0].rearrange("p n t -> p (n t)").bitcast(I32))
-        load_filled(nc.gpsimd, w0_s, w0_scales, 0)
-        load_filled(nc.gpsimd, w0_s, w0_scales, 1)
-        load_filled(nc.gpsimd, w0_s, w0_scales, 2)
-        load_rows(nc.sync, w_s, w_scales, 0)
-        load_rows(nc.sync, w_s, w_scales, 1)
-        load_rows(nc.sync, w_s, w_scales, 2)
-        load_rows(nc.sync, w_s, w_scales, 3)
+        nc.sync.dma_start(idx_o[:], offs2)
+        load_pair(nc.sync, w0_s, w0_scales, 0)
+        load_pair(nc.sync, w0_s, w0_scales, 1)
         nc.sync.dma_start(xo_w[:].bitcast(I32), xo_words[0].bitcast(I32))
         load_rows(nc.sync, xo_s, xo_scales, 0)
         load_rows(nc.sync, xo_s, xo_scales, 1)
         load_rows(nc.sync, xo_s, xo_scales, 2)
-        load_rows(nc.sync, xo_s, xo_scales, 3)
-        load_filled(nc.sync, w0_s, w0_scales, 3)
         nc.sync.dma_start(idx_a[:], offs3)
+        nc.sync.dma_start(idx_b[:], offs4)
+        load_rows(nc.sync, xo_s, xo_scales, 3)
         nc.sync.dma_start(ca_t[0][:], ca[0:P, :])
         nc.sync.dma_start(ca_t[1][:], ca[P : 2 * P, :])
-        nc.sync.dma_start(idx_b[:], offs4)
         nc.sync.dma_start(cb_t[0][:], cb[0:P, :])
         nc.sync.dma_start(cb_t[1][:], cb[P : 2 * P, :])
-        nc.sync.dma_start(wb_w[:].bitcast(I32), wb_words[0].rearrange("p n t -> p (n t)").bitcast(I32))
-        load_steps(nc, nc.sync, sa_t, sa)
         load_rows(nc.sync, wb_s, wb_scales, 0)
         load_rows(nc.sync, wb_s, wb_scales, 1)
         load_rows(nc.sync, wb_s, wb_scales, 2)
         load_rows(nc.sync, wb_s, wb_scales, 3)
-        load_steps(nc, nc.sync, sb_t, sb)
+        nc.gpsimd.dma_start(wb_w[:].bitcast(I32), wb_words[0].rearrange("p n t -> p (n t)").bitcast(I32))
+        load_steps(nc, nc.gpsimd, sa_t, sa)
+        load_steps(nc, nc.gpsimd, sb_t, sb)
 
         w_wd = sb_tile("w_wd", [P, PACK, P], U16)
         w_sd = sb_tile("w_sd", [P, PACK, P], U8)
@@ -141,13 +138,15 @@ def tile_list_gainandshift_kernel(
         xo_sg = sb_tile("xo_sg", [P, J], U8)
 
         nc.vector.tensor_copy(xt_sg[:], xt_s[:].indirect(idx_t[:]))
+        lift(nc, w_s)
+        nc.vector.tensor_copy(w_sd[:], dealt(w_s[:, 0, :]))
         nc.vector.tensor_copy(xt_wg[:], xt_w[:].indirect(idx_t[:]))
         nc.scalar.copy(w_wd[:].rearrange("p t m -> p m t"), w_w[:].rearrange("p (m t) -> p m t", t=PACK))
-        nc.vector.tensor_copy(w_sd[:], dealt(w_s[:]))
+        lift(nc, w0_s)
         nc.vector.tensor_copy(xo_wg[:], xo_w[:].indirect(idx_o[:]))
-        nc.vector.tensor_copy(xo_sg[:], xo_s[:].indirect(idx_o[:]))
+        nc.vector.tensor_copy(w0_sd[:], dealt(w0_s[:, 0, :]))
         nc.scalar.copy(w0_wd[:].rearrange("p t m -> p m t"), w0_w[:].rearrange("p (m t) -> p m t", t=PACK))
-        nc.vector.tensor_copy(w0_sd[:], dealt(w0_s[:]))
+        nc.vector.tensor_copy(xo_sg[:], xo_s[:].indirect(idx_o[:]))
 
         a_ps = [psum.tile([P, PACK, HALF], F32, name="a_ps%d" % h) for h in range(2)]
         p_ps = [psum.tile([P, 2, HALF], F32, name="p_ps%d" % h) for h in range(2)]
@@ -181,12 +180,12 @@ def tile_list_gainandshift_kernel(
             nc.vector.tensor_copy(ca_g[n][:], ca_t[n][:].indirect(idx_a[:]))
         for h in range(2):
             nc.scalar.activation(hid[h][:], a_ps[h][:].rearrange("p t j -> p j t"), ACT.Relu)
-        for n in range(2):
-            nc.vector.tensor_copy(cb_g[n][:], cb_t[n][:].indirect(idx_b[:]))
         for h in range(2):
             nc.vector.quantize_mx(
                 out=hid_w[h][:].bitcast(E4M3X4), scales=hid_s[h][:], in_=hid[h][:].rearrange("p j t -> p (j t)")
             )
+        for n in range(2):
+            nc.vector.tensor_copy(cb_g[n][:], cb_t[n][:].indirect(idx_b[:]))
         for n in range(2):
             nc.scalar.activation(looked_up[:, n * J : (n + 1) * J], ca_g[n][:].bitcast(E4M3), ACT.Copy, scale=sa_t[:, n : n + 1])
         for n in range(2):

from contextlib import ExitStack

import concourse.mybir as mybir

K, T, J, R, F, Z, V, D, N = 512, 1024, 256, 512, 512, 1024, 1024, 512, 256
FLOPS = 2 * (K * R * J + F * R * J + R * N * J)

F32 = mybir.dt.float32
BF16 = mybir.dt.bfloat16
I32 = mybir.dt.int32
U32 = mybir.dt.uint32
U16 = mybir.dt.uint16
U8 = mybir.dt.uint8
E4M3 = mybir.dt.float8_e4m3fn
E4M3X4 = mybir.dt.float8_e4m3fn_x4
E5M2X4 = mybir.dt.float8_e5m2_x4
E2M1X4 = mybir.dt.float4_e2m1fn_x4
ACT = mybir.ActivationFunctionType
ALU = mybir.AluOpType

P = 128
PACK = 4
HALF = J // 2


def load_filled(queue, plane, scales, q):
    rows = scales[0, 4 * q : 4 * q + 4, :].bitcast(I32)
    queue.dma_start(plane[32 * q : 32 * q + 32, :].bitcast(I32), rows.unsqueeze(0).broadcast_to([8, 4, rows.shape[1]]))


def load_rows(queue, plane, scales, q):
    queue.dma_start(plane[32 * q : 32 * q + 4, :].bitcast(I32), scales[0, 4 * q : 4 * q + 4, :].bitcast(I32))


def load_pair(queue, stage, scales, q):
    rows = scales[0].bitcast(I32).rearrange("(u q r) c -> q r u c", u=2, q=2)
    queue.dma_start(stage[32 * q : 32 * q + 4, :, :].bitcast(I32), rows[q])


def load_staged(queue, stage, scales):
    queue.dma_start(stage[0:4, :, :].bitcast(I32), scales[0].bitcast(I32).rearrange("(q r) c -> r q c", r=4))


def load_steps(nc, queue, tile, steps):
    with nc.allow_non_contiguous_dma(reason="one step a partition"):
        queue.dma_start(tile[:], steps.rearrange("(n p) o -> p (n o)", p=P))


def lift(nc, stage):
    nc.vector.tensor_copy(stage[64:128, 0, :].bitcast(I32), stage[0:64, 1, :].bitcast(I32))


def spread(nc, plane, stage, quadrants):
    for q in quadrants:
        nc.vector.tensor_copy(plane[32 * q : 32 * q + 4, :].bitcast(I32), stage[0:4, q, :].bitcast(I32))


def tile_list_gainandshift_kernel(
    tc, xt_words, xt_scales, xo_words, xo_scales, w_words, w_scales, w0_words, w0_scales,
    wb_words, wb_scales, ca, cb, sa, sb, offs, offs2, offs3, offs4, out,
):
    nc = tc.nc
    with ExitStack() as ctx:
        lists = ctx.enter_context(tc.tile_pool(name="lists", bufs=1))
        keep = ctx.enter_context(tc.tile_pool(name="keep", bufs=1))
        psum = ctx.enter_context(tc.psum_pool(name="psum", bufs=1))

        def sb_tile(name, shape, dtype, tag=None):
            return keep.tile(shape, dtype, name=name, tag=tag or name, align_bytes=64)

        idx_t = lists.tile([P, J // 16], U16, name="idx_t")
        idx_o = lists.tile([P, J // 16], U16, name="idx_o")
        idx_a = lists.tile([P, J // 16], U16, name="idx_a")
        idx_b = lists.tile([P, J // 16], U16, name="idx_b")

        xt_w = sb_tile("xt_w", [P, T], U32)
        xt_s = sb_tile("xt_s", [P, T], U8)
        xo_w = sb_tile("xo_w", [P, Z], U16, tag="xo_then_w0")
        xo_s = sb_tile("xo_s", [P, Z], U8)
        w_w = sb_tile("w_w", [P, R], U16)
        w_s = sb_tile("w_s", [P, 2, R], U8)
        w0_w = sb_tile("w0_w", [P, R], U32)
        w0_s = sb_tile("w0_s", [P, 2, R], U8)
        wb_w = sb_tile("wb_w", [P, N], U32)
        wb_s = sb_tile("wb_s", [P, N], U8)
        ca_t = [sb_tile("ca_%d" % n, [P, V], U8) for n in range(2)]
        cb_t = [sb_tile("cb_%d" % n, [P, D], U8) for n in range(2)]
        sa_t = sb_tile("sa_t", [P, 2], F32)
        sb_t = sb_tile("sb_t", [P, 2], F32)

        nc.vector.memset(w_s[:].rearrange("p u c -> p (u c)").bitcast(I32), 0)
        nc.vector.memset(w0_s[:].rearrange("p u c -> p (u c)").bitcast(I32), 0)
        nc.vector.memset(xo_s[:].bitcast(I32), 0)

        nc.sync.dma_start(idx_t[:], offs)
        load_filled(nc.scalar, xt_s, xt_scales, 2)
        load_filled(nc.sync, xt_s, xt_scales, 0)
        load_filled(nc.scalar, xt_s, xt_scales, 3)
        load_filled(nc.sync, xt_s, xt_scales, 1)
        load_pair(nc.scalar, w_s, w_scales, 0)
        load_pair(nc.sync, w_s, w_scales, 1)
        nc.sync.dma_start(xt_w[:].bitcast(I32), xt_words[0].rearrange("p n t -> p (n t)").bitcast(I32))
        nc.gpsimd.dma_start(w_w[:].bitcast(I32), w_words[0].bitcast(I32))
        nc.gpsimd.dma_start(w0_w[:].bitcast(I32), w0_words[0].rearrange("p n t -> p (n t)").bitcast(I32))
        nc.sync.dma_start(idx_o[:], offs2)
        load_pair(nc.sync, w0_s, w0_scales, 0)
        load_pair(nc.sync, w0_s, w0_scales, 1)
        nc.sync.dma_start(xo_w[:].bitcast(I32), xo_words[0].bitcast(I32))
        load_rows(nc.sync, xo_s, xo_scales, 0)
        load_rows(nc.sync, xo_s, xo_scales, 1)
        load_rows(nc.sync, xo_s, xo_scales, 2)
        nc.sync.dma_start(idx_a[:], offs3)
        nc.sync.dma_start(idx_b[:], offs4)
        load_rows(nc.sync, xo_s, xo_scales, 3)
        nc.sync.dma_start(ca_t[0][:], ca[0:P, :])
        nc.sync.dma_start(ca_t[1][:], ca[P : 2 * P, :])
        nc.sync.dma_start(cb_t[0][:], cb[0:P, :])
        nc.sync.dma_start(cb_t[1][:], cb[P : 2 * P, :])
        load_rows(nc.sync, wb_s, wb_scales, 0)
        load_rows(nc.sync, wb_s, wb_scales, 1)
        load_rows(nc.sync, wb_s, wb_scales, 2)
        load_rows(nc.sync, wb_s, wb_scales, 3)
        nc.gpsimd.dma_start(wb_w[:].bitcast(I32), wb_words[0].rearrange("p n t -> p (n t)").bitcast(I32))
        load_steps(nc, nc.gpsimd, sa_t, sa)
        load_steps(nc, nc.gpsimd, sb_t, sb)

        w_wd = sb_tile("w_wd", [P, PACK, P], U16)
        w_sd = sb_tile("w_sd", [P, PACK, P], U8)
        w0_wd = sb_tile("w0_wd", [P, PACK, P], U32, tag="w0_then_steps")
        w0_sd = sb_tile("w0_sd", [P, PACK, P], U8, tag="xo_then_w0")

        def dealt(rows):
            return rows.rearrange("p (m t) -> p t m", t=PACK)

        xt_wg = sb_tile("xt_wg", [P, J], U32)
        xt_sg = sb_tile("xt_sg", [P, J], U8)
        xo_wg = sb_tile("xo_wg", [P, J], U16)
        xo_sg = sb_tile("xo_sg", [P, J], U8)

        nc.vector.tensor_copy(xt_sg[:], xt_s[:].indirect(idx_t[:]))
        lift(nc, w_s)
        nc.vector.tensor_copy(w_sd[:], dealt(w_s[:, 0, :]))
        nc.vector.tensor_copy(xt_wg[:], xt_w[:].indirect(idx_t[:]))
        nc.scalar.copy(w_wd[:].rearrange("p t m -> p m t"), w_w[:].rearrange("p (m t) -> p m t", t=PACK))
        lift(nc, w0_s)
        nc.vector.tensor_copy(xo_wg[:], xo_w[:].indirect(idx_o[:]))
        nc.vector.tensor_copy(w0_sd[:], dealt(w0_s[:, 0, :]))
        nc.scalar.copy(w0_wd[:].rearrange("p t m -> p m t"), w0_w[:].rearrange("p (m t) -> p m t", t=PACK))
        nc.vector.tensor_copy(xo_sg[:], xo_s[:].indirect(idx_o[:]))

        a_ps = [psum.tile([P, PACK, HALF], F32, name="a_ps%d" % h) for h in range(2)]
        p_ps = [psum.tile([P, 2, HALF], F32, name="p_ps%d" % h) for h in range(2)]
        halves = [slice(h * HALF, (h + 1) * HALF) for h in range(2)]

        for h in range(2):
            for t in range(PACK):
                nc.tensor.matmul_mx(
                    out=a_ps[h][:, t, :], lhsT=w_wd[:, t, :].bitcast(E2M1X4), lhsT_scale=w_sd[:, t, :],
                    rhs=xt_wg[:, halves[h]].bitcast(E4M3X4), rhs_scale=xt_sg[:, halves[h]],
                    start=(t == 0), stop=False,
                )
        for h in range(2):
            for t in range(PACK):
                nc.tensor.matmul_mx(
                    out=a_ps[h][:, t, :], lhsT=w0_wd[:, t, :].bitcast(E5M2X4), lhsT_scale=w0_sd[:, t, :],
                    rhs=xo_wg[:, halves[h]].bitcast(E2M1X4), rhs_scale=xo_sg[:, halves[h]],
                    start=False, stop=(t == PACK - 1),
                )

        ca_g = [sb_tile("ca_g%d" % n, [P, J], U8) for n in range(2)]
        cb_g = [sb_tile("cb_g%d" % n, [P, J], U8) for n in range(2)]
        looked_up = sb_tile("looked_up", [P, 4 * J], F32, tag="w0_then_steps")
        gain = looked_up[:, 0 : 2 * J].rearrange("p (n j) -> p n j", n=2)
        shift = looked_up[:, 2 * J : 4 * J].rearrange("p (n j) -> p n j", n=2)
        hid = [sb_tile("hid%d" % h, [P, HALF, PACK], BF16) for h in range(2)]
        hid_w = [sb_tile("hid_w%d" % h, [P, HALF], U32) for h in range(2)]
        hid_s = [sb_tile("hid_s%d" % h, [P, HALF], U8) for h in range(2)]

        for n in range(2):
            nc.vector.tensor_copy(ca_g[n][:], ca_t[n][:].indirect(idx_a[:]))
        for h in range(2):
            nc.scalar.activation(hid[h][:], a_ps[h][:].rearrange("p t j -> p j t"), ACT.Relu)
        for h in range(2):
            nc.vector.quantize_mx(
                out=hid_w[h][:].bitcast(E4M3X4), scales=hid_s[h][:], in_=hid[h][:].rearrange("p j t -> p (j t)")
            )
        for n in range(2):
            nc.vector.tensor_copy(cb_g[n][:], cb_t[n][:].indirect(idx_b[:]))
        for n in range(2):
            nc.scalar.activation(looked_up[:, n * J : (n + 1) * J], ca_g[n][:].bitcast(E4M3), ACT.Copy, scale=sa_t[:, n : n + 1])
        for n in range(2):
            nc.scalar.activation(looked_up[:, (2 + n) * J : (3 + n) * J], cb_g[n][:].bitcast(E4M3), ACT.Copy, scale=sb_t[:, n : n + 1])

        for h in range(2):
            for n in range(2):
                cols = slice(n * P, (n + 1) * P)
                nc.tensor.matmul_mx(
                    out=p_ps[h][:, n, :], lhsT=wb_w[:, cols].bitcast(E5M2X4), lhsT_scale=wb_s[:, cols],
                    rhs=hid_w[h][:].bitcast(E4M3X4), rhs_scale=hid_s[h][:], start=True, stop=True,
                )

        out_v = out.rearrange("(n p) j -> p n j", p=P)
        scaled = [sb_tile("scaled%d" % h, [P, 2, HALF], F32) for h in range(2)]
        result = [sb_tile("result%d" % h, [P, 2, HALF], F32) for h in range(2)]
        for h in range(2):
            nc.vector.tensor_tensor(scaled[h][:], p_ps[h][:], gain[:, :, halves[h]], ALU.mult)
        for h in range(2):
            nc.vector.tensor_tensor(result[h][:], scaled[h][:], shift[:, :, halves[h]], ALU.add)
            nc.sync.dma_start(out_v[:, :, halves[h]], result[h][:])
